import numpy as np
import ml_dtypes


def mxq(x, axis, fmt="e4m3"):
    dtype, down = {"e4m3": (ml_dtypes.float8_e4m3fn, 7), "e5m2": (ml_dtypes.float8_e5m2, 14)}[fmt]
    v = np.moveaxis(np.asarray(x, np.float32).astype(ml_dtypes.bfloat16).astype(np.float64), axis, -1)
    blocks = v.reshape(v.shape[:-1] + (-1, 32))
    amax = np.abs(blocks).max(-1, keepdims=True)
    byte = np.maximum(np.where(amax > 0, np.frexp(amax)[1] - 1 + 127, 0) - down, 1)
    scale = np.exp2(byte - 127.0)
    codes = (blocks / scale).astype(np.float32).astype(dtype).astype(np.float64)
    return np.moveaxis((codes * scale).reshape(v.shape), -1, axis)


WIDE = False


def mx_kscale(k):
    if not WIDE:
        return np.ones(k)
    levels = np.array([10, -10, 5, -5, 0])
    if k % 512:
        return np.exp2(np.random.permutation(np.resize(levels, k // 32))).repeat(32)
    a = np.empty((k // 512, 16))
    for p in range(k // 512):
        a[p, :8] = np.random.permutation(np.resize(levels, 8))
        for g in range(8):
            far = levels[np.abs(levels - a[p, g]) >= 10]
            a[p, g + 8] = far[np.random.randint(len(far))]
    return np.exp2(a.ravel()).repeat(32)


def f64(x):
    return np.asarray(x).astype(np.float64)


def striped8(idx):
    return np.asarray(idx).reshape(8, -1, 16).transpose(0, 2, 1).reshape(128, -1).astype(np.uint16)


def unstriped8(offs):
    return offs.reshape(8, 16, -1).transpose(0, 2, 1).reshape(8, -1).astype(np.int64)


def pick8(x, idx, run):
    r = np.arange(len(x))
    return x[r[:, None], idx[r % (8 * run) // run]]


E2M1 = np.array([0.0, 0.5, 1.0, 1.5, 2.0, 3.0, 4.0, 6.0, -0.0, -0.5, -1.0, -1.5, -2.0, -3.0, -4.0, -6.0])


def pack_weight(w, fmt):
    k, n = w.shape
    w = f64(np.asarray(w, np.float32).astype(ml_dtypes.bfloat16)).reshape(k // 32, 32, n)
    amax = np.abs(w).max(1)
    if fmt == "e4m3":
        byte = np.frexp(amax)[1] - 1 + 127 - 7
    else:
        mant, ex = np.frexp(amax / 6.0)
        byte = np.where(mant > 0.5, ex, ex - 1) + 127
    byte = np.clip(np.where(amax > 0, byte, 1), 1, 254)
    scaled = (w * np.exp2(127.0 - byte)[:, None, :]).reshape(k, n).astype(np.float32)
    by_word = np.ascontiguousarray(scaled.reshape(k // 512, 128, 4, n).transpose(0, 1, 3, 2))
    if fmt == "e4m3":
        words = by_word.astype(ml_dtypes.float8_e4m3fn).view(np.uint8)
    else:
        c = by_word.astype(ml_dtypes.float4_e2m1fn).view(np.uint8) & 0xF
        words = (c[..., 0::2] | (c[..., 1::2] << 4)).reshape(k // 512, 128, 2 * n)
    return np.ascontiguousarray(words), np.ascontiguousarray(byte.astype(np.uint8).reshape(k // 512, 16, n))


def unpack_weight(words, scales, fmt):
    g, _, n = scales.shape
    words = np.ascontiguousarray(words).reshape(g, 128, n, -1)
    if fmt == "e4m3":
        vals = words.view(ml_dtypes.float8_e4m3fn).astype(np.float64)
    else:
        nib = np.empty((g, 128, n, 4), np.uint8)
        nib[..., 0::2] = words & 0xF
        nib[..., 1::2] = words >> 4
        vals = E2M1[nib]
    vals = vals * np.repeat(np.exp2(scales.astype(np.float64) - 127.0), 8, axis=1)[..., None]
    return vals.transpose(0, 1, 3, 2).reshape(g * 512, n)


D, E, T, Q, I = 512, 512, 1024, 128, 256


def setup_inputs():
    n = np.random.standard_normal
    idx = np.stack([np.random.permutation(T)[:I] for _ in range(8)])
    fd = mx_kscale(D)
    fe = mx_kscale(E)
    keysp = pack_weight(n((D, T)) / fd[:, None], "e4m3")
    return {
        "query": (n((D, Q)) * 0.6 / np.sqrt(D) * fd[:, None]).astype(np.float32),
        "keys_words": keysp[0],
        "keys_scales": keysp[1],
        "gout": (n((E, Q)) * 1 / np.sqrt(E) * fe[:, None]).astype(np.float32),
        "vals": (n((E, T)) / fe[:, None]).astype(np.float32),
        "zp": (np.random.uniform(200.0, 800.0, (Q, 1))).astype(np.float32),
        "cp": (np.random.uniform(-100.0, 100.0, (Q, 1))).astype(np.float32),
        "old": (0.5 * n((Q, T))).astype(np.float32),
        "offs": striped8(idx),
    }


def reference(query, keys_words, keys_scales, gout, vals, zp, cp, old, offs):
    idx = unstriped8(offs)
    keysu = unpack_weight(keys_words, keys_scales, "e4m3")
    queryq = mxq(f64(query), 0, "e4m3")
    a = queryq.T @ keysu
    p = np.exp(pick8(a, idx, 16))
    z = np.sum(p, axis=1, keepdims=True) + f64(zp)
    goutq = mxq(f64(gout), 0, "e4m3")
    valsq = mxq(f64(vals), 0, "e4m3")
    c0 = goutq.T @ valsq
    dz = (np.sum(p * pick8(c0, idx, 16), axis=1, keepdims=True) + f64(cp)) / np.square(z) * (-1.0)
    dp = 1.0 / z * pick8(c0, idx, 16) + dz
    e1 = dp * p
    s1 = np.zeros((Q, T))
    s1[np.arange(Q)[:, None], idx[np.arange(Q) % 128 // 16]] = e1
    y = s1 * 1024.0 + f64(old)
    return y

@@ -1,0 +1,192 @@
+from contextlib import ExitStack
+
+import concourse.mybir as mybir
+
+D, E, T, Q, SLOTS = 512, 512, 1024, 128, 256
+FLOPS = 2 * Q * T * (D + E)
+
+F32 = mybir.dt.float32
+BF16 = mybir.dt.bfloat16
+I32 = mybir.dt.int32
+U32 = mybir.dt.uint32
+U16 = mybir.dt.uint16
+U8 = mybir.dt.uint8
+FP8X4 = mybir.dt.float8_e4m3fn_x4
+ALU = mybir.AluOpType
+ACT = mybir.ActivationFunctionType
+
+P = 128
+PACK = 4
+GAIN = 1024.0
+VAL_CHUNKS = (256, 256, 256, 256)
+VECTOR_COLS = (160, 160, 160, 160)
+KEY_CHUNKS = (512, 256, 256)
+STORE_CHUNKS = (256, 256, 256, 256)
+
+
+def interleave(copy, grouped, raw, c0, c1):
+    copy(
+        out=grouped[:, c0:c1, :].rearrange("p (c i) t -> p c t i", i=4),
+        in_=raw[:, :, c0:c1].rearrange("p t (c i) -> p c t i", i=4),
+    )
+
+
+def spans(widths):
+    return [slice(sum(widths[:n]), sum(widths[: n + 1])) for n in range(len(widths))]
+
+
+def tile_attend_bsharedprefix_heads_kernel(tc, query, keys_words, keys_scales, gout, vals, zp, cp, old, offs, out):
+    nc = tc.nc
+    with ExitStack() as ctx:
+        keep = ctx.enter_context(tc.tile_pool(name="keep", bufs=1))
+        psum = ctx.enter_context(tc.psum_pool(name="psum", bufs=1))
+
+        offsets = keep.tile([P, SLOTS // 16], U16, name="offsets")
+        key_scales = keep.tile([P, T], U8, name="key_scales", align_bytes=64)
+        placed = keep.tile([P, T], F32, name="placed")
+        p_ext = keep.tile([P, SLOTS + 4], F32, name="p_ext")
+        c_ext = keep.tile([P, SLOTS + 4], F32, name="c_ext")
+        q_raw = keep.tile([P, PACK, Q], F32, name="q_raw")
+        g_raw = keep.tile([P, PACK, Q], F32, name="g_raw")
+        val_cols = spans(VAL_CHUNKS)
+        key_cols = spans(KEY_CHUNKS)
+        key_codes = [keep.tile([P, w], U32, name="key_codes%d" % n, align_bytes=64) for n, w in enumerate(KEY_CHUNKS)]
+        v_raw = [keep.tile([P, PACK, w], F32, name="v_raw%d" % n) for n, w in enumerate(VAL_CHUNKS)]
+        old_sb = keep.tile([P, T], F32, name="old_sb")
+
+        nc.vector.memset(key_scales[:].bitcast(I32), 0)
+        nc.vector.memset(placed[:], 0.0)
+        nc.gpsimd.memset(p_ext[:, SLOTS:], 1.0)
+        nc.gpsimd.memset(c_ext[:, SLOTS:], 0.0)
+
+        def load_vals(n):
+            nc.sync.dma_start(out=v_raw[n][:], in_=vals[:, val_cols[n]].rearrange("(p j) w -> p j w", j=PACK))
+
+        key_words = keys_words[0].rearrange("p n t -> p (n t)").bitcast(I32)
+
+        def load_keys(n):
+            nc.sync.dma_start(out=key_codes[n][:].bitcast(I32), in_=key_words[:, key_cols[n]])
+
+        def load_scales():
+            for quad in range(4):
+                nc.sync.dma_start(
+                    out=key_scales[32 * quad : 32 * quad + 4, :].bitcast(I32),
+                    in_=keys_scales[0, 4 * quad : 4 * quad + 4, :].bitcast(I32),
+                )
+
+        def load_prefix():
+            with nc.allow_non_contiguous_dma(reason="one value a partition"):
+                nc.gpsimd.dma_start(out=p_ext[:, SLOTS : SLOTS + 1], in_=zp)
+                nc.gpsimd.dma_start(out=c_ext[:, SLOTS + 1 : SLOTS + 2], in_=cp)
+
+        load_prefix()
+        nc.sync.dma_start(out=g_raw[:], in_=gout.rearrange("(p j) w -> p j w", j=PACK))
+        nc.sync.dma_start(out=q_raw[:], in_=query.rearrange("(p j) w -> p j w", j=PACK))
+        load_vals(0)
+        nc.sync.dma_start(offsets[:], offs)
+        load_scales()
+        load_keys(0)
+        load_vals(1)
+        load_vals(2)
+        load_vals(3)
+        load_keys(1)
+        load_keys(2)
+        nc.sync.dma_start(out=old_sb[:], in_=old)
+
+        def operand(name, width):
+            grouped = keep.tile([P, width, PACK], BF16, name=name + "_grouped", align_bytes=64)
+            codes = keep.tile([P, width], U32, name=name + "_codes", align_bytes=64)
+            scales = keep.tile([P, width], U8, name=name + "_scales", align_bytes=64)
+            return grouped, codes, scales
+
+        def quantize(grouped, codes, scales):
+            nc.vector.quantize_mx(
+                out=codes[:].bitcast(FP8X4), scales=scales[:], in_=grouped[:].rearrange("p w j -> p (w j)")
+            )
+
+        g_op = operand("g", Q)
+        q_op = operand("q", Q)
+        c_all = keep.tile([P, T], F32, name="c_all")
+        a_all = keep.tile([P, T], F32, name="a_all")
+
+        def stationary(op, raw, copy):
+            interleave(copy, op[0], raw, 0, Q)
+            quantize(*op)
+
+        v_ops = [operand("v%d" % n, w) for n, w in enumerate(VAL_CHUNKS)]
+
+        def value_prepare(n):
+            w = VAL_CHUNKS[n]
+            grouped, codes, scales = v_ops[n]
+            split = VECTOR_COLS[n]
+            interleave(nc.vector.tensor_copy, grouped, v_raw[n], 0, split)
+            if split < w:
+                interleave(nc.scalar.copy, grouped, v_raw[n], split, w)
+            quantize(grouped, codes, scales)
+
+        def value_chunk(n, drain):
+            w = VAL_CHUNKS[n]
+            grouped, codes, scales = v_ops[n]
+            acc = psum.tile([P, w], F32, name="c_acc%d" % (n % 4))
+            nc.tensor.matmul_mx(
+                out=acc[:], lhsT=g_op[1][:].bitcast(FP8X4), lhsT_scale=g_op[2][:],
+                rhs=codes[:].bitcast(FP8X4), rhs_scale=scales[:], start=True, stop=True,
+            )
+            drain(out=c_all[:, val_cols[n]], in_=acc[:])
+
+        def key_chunk(n, drain):
+            acc = psum.tile([P, KEY_CHUNKS[n]], F32, name="a_acc%d" % n)
+            nc.tensor.matmul_mx(
+                out=acc[:], lhsT=q_op[1][:].bitcast(FP8X4), lhsT_scale=q_op[2][:],
+                rhs=key_codes[n][:].bitcast(FP8X4), rhs_scale=key_scales[:, key_cols[n]], start=True, stop=True,
+            )
+            drain(out=a_all[:, key_cols[n]], in_=acc[:])
+
+        def look_up_c():
+            nc.vector.tensor_copy(out=c_ext[:, :SLOTS], in_=c_all[:].indirect(offsets[:]))
+
+        stationary(g_op, g_raw, nc.vector.tensor_copy)
+        stationary(q_op, q_raw, nc.scalar.copy)
+        value_prepare(0)
+        value_chunk(0, nc.scalar.copy)
+        key_chunk(0, nc.scalar.copy)
+        value_prepare(1)
+        value_chunk(1, nc.scalar.copy)
+        value_prepare(2)
+        value_chunk(2, nc.scalar.copy)
+        value_prepare(3)
+        key_chunk(1, nc.scalar.copy)
+        key_chunk(2, nc.scalar.copy)
+        value_chunk(3, nc.vector.tensor_copy)
+        look_up_c()
+
+
+        nc.scalar.activation(out=p_ext[:, :SLOTS], in_=a_all[:].indirect(offsets[:]), func=ACT.Exp)
+
+        z = keep.tile([P, 1], F32, name="z")
+        inv_z = keep.tile([P, 1], F32, name="inv_z")
+        neg_m = keep.tile([P, 1], F32, name="neg_m")
+        z_terms = keep.tile([P, SLOTS + 1], F32, name="z_terms")
+        m_terms = keep.tile([P, SLOTS + 2], F32, name="m_terms")
+        centred = keep.tile([P, SLOTS], F32, name="centred")
+        weight = keep.tile([P, SLOTS], F32, name="weight")
+        nc.scalar.activation(out=z_terms[:], in_=p_ext[:, : SLOTS + 1], func=ACT.Copy, accum_out=z[:])
+        nc.vector.scalar_tensor_tensor(
+            out=m_terms[:], in0=p_ext[:, : SLOTS + 2], scalar=-1.0, in1=c_ext[:, : SLOTS + 2],
+            op0=ALU.mult, op1=ALU.mult, accum_out=neg_m[:],
+        )
+        nc.vector.reciprocal(out=inv_z[:], in_=z[:])
+        nc.scalar.activation(
+            out=centred[:], in_=c_ext[:, :SLOTS], func=ACT.Identity, scale=z[:], bias=neg_m[:]
+        )
+        nc.vector.tensor_scalar(
+            out=weight[:], in0=p_ext[:, :SLOTS], scalar1=inv_z[:], scalar2=inv_z[:], op0=ALU.mult, op1=ALU.mult
+        )
+        nc.vector.tensor_tensor(out=placed[:].indirect(offsets[:]), in0=centred[:], in1=weight[:], op=ALU.mult)
+
+        for n, cols in enumerate(spans(STORE_CHUNKS)):
+            result = keep.tile([P, STORE_CHUNKS[n]], F32, name="result%d" % n)
+            nc.vector.scalar_tensor_tensor(
+                out=result[:], in0=placed[:, cols], scalar=GAIN, in1=old_sb[:, cols], op0=ALU.mult, op1=ALU.add
+            )
+            (nc.sync if n % 2 == 0 else nc.scalar).dma_start(out=out[:, cols], in_=result[:])

@@ -18,9 +18,12 @@ ACT = mybir.ActivationFunctionType
 P = 128
 PACK = 4
 GAIN = 1024.0
-VAL_CHUNKS = (256, 256, 256, 256)
-VECTOR_COLS = (160, 160, 160, 160)
-KEY_CHUNKS = (512, 256, 256)
+VAL_CHUNKS = (256, 256, 256, 128, 128)
+VECTOR_COLS = (256, 256, 256, 128, 128)
+KEY_CHUNKS = (512, 512)
+C_BANKS = ("c0", "c1", "c2", "c3", "c4")
+A_BANKS = ("a0", "a1")
+CODE_TAGS = {}
 STORE_CHUNKS = (256, 256, 256, 256)
 
 
@@ -50,10 +53,11 @@ def tile_attend_bsharedprefix_heads_kernel(tc, query, keys_words, keys_scales, g
         g_raw = keep.tile([P, PACK, Q], F32, name="g_raw")
         val_cols = spans(VAL_CHUNKS)
         key_cols = spans(KEY_CHUNKS)
-        key_codes = [keep.tile([P, w], U32, name="key_codes%d" % n, align_bytes=64) for n, w in enumerate(KEY_CHUNKS)]
+        key_codes = keep.tile([P, T], U32, name="key_codes", align_bytes=64)
         v_raw = [keep.tile([P, PACK, w], F32, name="v_raw%d" % n) for n, w in enumerate(VAL_CHUNKS)]
         old_sb = keep.tile([P, T], F32, name="old_sb")
 
+        scale_rows = keep.tile([P, T // 4], I32, name="scale_rows")
         nc.vector.memset(key_scales[:].bitcast(I32), 0)
         nc.vector.memset(placed[:], 0.0)
         nc.gpsimd.memset(p_ext[:, SLOTS:], 1.0)
@@ -65,12 +69,12 @@ def tile_attend_bsharedprefix_heads_kernel(tc, query, keys_words, keys_scales, g
         key_words = keys_words[0].rearrange("p n t -> p (n t)").bitcast(I32)
 
         def load_keys(n):
-            nc.sync.dma_start(out=key_codes[n][:].bitcast(I32), in_=key_words[:, key_cols[n]])
+            nc.sync.dma_start(out=key_codes[:].bitcast(I32), in_=key_words)
 
         def load_scales():
             for quad in range(4):
                 nc.sync.dma_start(
-                    out=key_scales[32 * quad : 32 * quad + 4, :].bitcast(I32),
+                    out=scale_rows[32 * quad : 32 * quad + 4, :],
                     in_=keys_scales[0, 4 * quad : 4 * quad + 4, :].bitcast(I32),
                 )
 
@@ -80,22 +84,25 @@ def tile_attend_bsharedprefix_heads_kernel(tc, query, keys_words, keys_scales, g
                 nc.gpsimd.dma_start(out=c_ext[:, SLOTS + 1 : SLOTS + 2], in_=cp)
 
         load_prefix()
-        nc.sync.dma_start(out=g_raw[:], in_=gout.rearrange("(p j) w -> p j w", j=PACK))
-        nc.sync.dma_start(out=q_raw[:], in_=query.rearrange("(p j) w -> p j w", j=PACK))
-        load_vals(0)
         nc.sync.dma_start(offsets[:], offs)
+        nc.sync.dma_start(out=q_raw[:], in_=query.rearrange("(p j) w -> p j w", j=PACK))
         load_scales()
         load_keys(0)
+        nc.sync.dma_start(out=g_raw[:], in_=gout.rearrange("(p j) w -> p j w", j=PACK))
+        load_vals(0)
         load_vals(1)
         load_vals(2)
         load_vals(3)
-        load_keys(1)
-        load_keys(2)
+        load_vals(4)
         nc.sync.dma_start(out=old_sb[:], in_=old)
 
-        def operand(name, width):
-            grouped = keep.tile([P, width, PACK], BF16, name=name + "_grouped", align_bytes=64)
-            codes = keep.tile([P, width], U32, name=name + "_codes", align_bytes=64)
+        for quad in range(4):
+            rows = slice(32 * quad, 32 * quad + 4)
+            nc.vector.tensor_copy(out=key_scales[rows, :].bitcast(I32), in_=scale_rows[rows, :])
+
+        def operand(name, width, codes_tag=None):
+            grouped = keep.tile([P, width, PACK], BF16, name=name + "_grouped", tag=name + "_grouped", align_bytes=64)
+            codes = keep.tile([P, width], U32, name=name + "_codes", tag=codes_tag or name + "_codes", align_bytes=64)
             scales = keep.tile([P, width], U8, name=name + "_scales", align_bytes=64)
             return grouped, codes, scales
 
@@ -113,21 +120,40 @@ def tile_attend_bsharedprefix_heads_kernel(tc, query, keys_words, keys_scales, g
             interleave(copy, op[0], raw, 0, Q)
             quantize(*op)
 
-        v_ops = [operand("v%d" % n, w) for n, w in enumerate(VAL_CHUNKS)]
+        v_ops = {}
 
         def value_prepare(n):
             w = VAL_CHUNKS[n]
+            v_ops[n] = operand("v%d" % n, w, CODE_TAGS.get(n))
             grouped, codes, scales = v_ops[n]
-            split = VECTOR_COLS[n]
-            interleave(nc.vector.tensor_copy, grouped, v_raw[n], 0, split)
-            if split < w:
-                interleave(nc.scalar.copy, grouped, v_raw[n], split, w)
-            quantize(grouped, codes, scales)
+            for half in range(2):
+                interleave(nc.vector.tensor_copy, grouped, v_raw[n], half * w // 2, (half + 1) * w // 2)
+
+        def value_quantize(n):
+            grouped, codes, scales = v_ops[n]
+            w = VAL_CHUNKS[n]
+            for half in range(2):
+                cols = slice(half * w // 2, (half + 1) * w // 2)
+                nc.vector.quantize_mx(
+                    out=codes[:, cols].bitcast(FP8X4), scales=scales[:, cols],
+                    in_=grouped[:, cols, :].rearrange("p w j -> p (w j)"),
+                )
+
+        def value_pair(n, drain):
+            w = VAL_CHUNKS[n]
+            acc = psum.tile([P, 2 * w], F32, name="acc", tag=C_BANKS[n])
+            for m in range(2):
+                grouped, codes, scales = v_ops[n + m]
+                nc.tensor.matmul_mx(
+                    out=acc[:, m * w : (m + 1) * w], lhsT=g_op[1][:].bitcast(FP8X4), lhsT_scale=g_op[2][:],
+                    rhs=codes[:].bitcast(FP8X4), rhs_scale=scales[:], start=True, stop=True,
+                )
+            drain(out=c_all[:, val_cols[n].start : val_cols[n + 1].stop], in_=acc[:])
 
         def value_chunk(n, drain):
             w = VAL_CHUNKS[n]
             grouped, codes, scales = v_ops[n]
-            acc = psum.tile([P, w], F32, name="c_acc%d" % (n % 4))
+            acc = psum.tile([P, w], F32, name="acc", tag=C_BANKS[n])
             nc.tensor.matmul_mx(
                 out=acc[:], lhsT=g_op[1][:].bitcast(FP8X4), lhsT_scale=g_op[2][:],
                 rhs=codes[:].bitcast(FP8X4), rhs_scale=scales[:], start=True, stop=True,
@@ -135,54 +161,65 @@ def tile_attend_bsharedprefix_heads_kernel(tc, query, keys_words, keys_scales, g
             drain(out=c_all[:, val_cols[n]], in_=acc[:])
 
         def key_chunk(n, drain):
-            acc = psum.tile([P, KEY_CHUNKS[n]], F32, name="a_acc%d" % n)
+            acc = psum.tile([P, KEY_CHUNKS[n]], F32, name="acc", tag=A_BANKS[n])
             nc.tensor.matmul_mx(
                 out=acc[:], lhsT=q_op[1][:].bitcast(FP8X4), lhsT_scale=q_op[2][:],
-                rhs=key_codes[n][:].bitcast(FP8X4), rhs_scale=key_scales[:, key_cols[n]], start=True, stop=True,
+                rhs=key_codes[:, key_cols[n]].bitcast(FP8X4), rhs_scale=key_scales[:, key_cols[n]], start=True, stop=True,
             )
             drain(out=a_all[:, key_cols[n]], in_=acc[:])
+
+        z = keep.tile([P, 1], F32, name="z")
+        z_terms = keep.tile([P, SLOTS + 1], F32, name="z_terms")
+
+        def exponentials():
+            nc.scalar.activation(out=p_ext[:, :SLOTS], in_=a_all[:].indirect(offsets[:]), func=ACT.Exp)
+            nc.scalar.activation(out=z_terms[:], in_=p_ext[:, : SLOTS + 1], func=ACT.Copy, accum_out=z[:])
 
         def look_up_c():
             nc.vector.tensor_copy(out=c_ext[:, :SLOTS], in_=c_all[:].indirect(offsets[:]))
 
-        stationary(g_op, g_raw, nc.vector.tensor_copy)
         stationary(q_op, q_raw, nc.scalar.copy)
-        value_prepare(0)
-        value_chunk(0, nc.scalar.copy)
         key_chunk(0, nc.scalar.copy)
+        key_chunk(1, nc.scalar.copy)
+        stationary(g_op, g_raw, nc.vector.tensor_copy)
+        exponentials()
+        value_prepare(0)
+        value_quantize(0)
+        value_chunk(0, nc.scalar.copy)
         value_prepare(1)
+        value_quantize(1)
         value_chunk(1, nc.scalar.copy)
         value_prepare(2)
+        value_quantize(2)
         value_chunk(2, nc.scalar.copy)
         value_prepare(3)
-        key_chunk(1, nc.scalar.copy)
-        key_chunk(2, nc.scalar.copy)
-        value_chunk(3, nc.vector.tensor_copy)
-        look_up_c()
+        value_quantize(3)
+        value_chunk(3, nc.scalar.copy)
+        value_prepare(4)
+        value_quantize(4)
+        value_chunk(4, nc.scalar.copy)
 
 
-        nc.scalar.activation(out=p_ext[:, :SLOTS], in_=a_all[:].indirect(offsets[:]), func=ACT.Exp)
-
-        z = keep.tile([P, 1], F32, name="z")
-        inv_z = keep.tile([P, 1], F32, name="inv_z")
+        inv_z = keep.tile([P, 1], F32, name="inv_z", tag="v4_grouped", align_bytes=64)
         neg_m = keep.tile([P, 1], F32, name="neg_m")
-        z_terms = keep.tile([P, SLOTS + 1], F32, name="z_terms")
         m_terms = keep.tile([P, SLOTS + 2], F32, name="m_terms")
         centred = keep.tile([P, SLOTS], F32, name="centred")
-        weight = keep.tile([P, SLOTS], F32, name="weight")
-        nc.scalar.activation(out=z_terms[:], in_=p_ext[:, : SLOTS + 1], func=ACT.Copy, accum_out=z[:])
+        weight = keep.tile([P, SLOTS + 2], F32, name="weight")
+        nc.vector.reciprocal(out=inv_z[:], in_=z[:])
+        nc.vector.tensor_scalar(
+            out=weight[:], in0=p_ext[:, : SLOTS + 2], scalar1=inv_z[:], scalar2=None, op0=ALU.mult
+        )
+        look_up_c()
         nc.vector.scalar_tensor_tensor(
-            out=m_terms[:], in0=p_ext[:, : SLOTS + 2], scalar=-1.0, in1=c_ext[:, : SLOTS + 2],
+            out=m_terms[:], in0=weight[:], scalar=-1.0, in1=c_ext[:, : SLOTS + 2],
             op0=ALU.mult, op1=ALU.mult, accum_out=neg_m[:],
         )
-        nc.vector.reciprocal(out=inv_z[:], in_=z[:])
-        nc.scalar.activation(
-            out=centred[:], in_=c_ext[:, :SLOTS], func=ACT.Identity, scale=z[:], bias=neg_m[:]
-        )
         nc.vector.tensor_scalar(
-            out=weight[:], in0=p_ext[:, :SLOTS], scalar1=inv_z[:], scalar2=inv_z[:], op0=ALU.mult, op1=ALU.mult
+            out=centred[:], in0=c_ext[:, :SLOTS], scalar1=neg_m[:], scalar2=None, op0=ALU.add
         )
-        nc.vector.tensor_tensor(out=placed[:].indirect(offsets[:]), in0=centred[:], in1=weight[:], op=ALU.mult)
+        nc.vector.tensor_tensor(
+            out=placed[:].indirect(offsets[:]), in0=centred[:], in1=weight[:, :SLOTS], op=ALU.mult
+        )
 
         for n, cols in enumerate(spans(STORE_CHUNKS)):
             result = keep.tile([P, STORE_CHUNKS[n]], F32, name="result%d" % n)

from contextlib import ExitStack

import concourse.mybir as mybir

D, E, T, Q, SLOTS = 512, 512, 1024, 128, 256
FLOPS = 2 * Q * T * (D + E)

F32 = mybir.dt.float32
BF16 = mybir.dt.bfloat16
I32 = mybir.dt.int32
U32 = mybir.dt.uint32
U16 = mybir.dt.uint16
U8 = mybir.dt.uint8
FP8X4 = mybir.dt.float8_e4m3fn_x4
ALU = mybir.AluOpType
ACT = mybir.ActivationFunctionType

P = 128
PACK = 4
GAIN = 1024.0
VAL_CHUNKS = (256, 256, 256, 128, 128)
VECTOR_COLS = (256, 256, 256, 128, 128)
KEY_CHUNKS = (512, 512)
C_BANKS = ("c0", "c1", "c2", "c3", "c4")
A_BANKS = ("a0", "a1")
CODE_TAGS = {}
STORE_CHUNKS = (256, 256, 256, 256)


def interleave(copy, grouped, raw, c0, c1):
    copy(
        out=grouped[:, c0:c1, :].rearrange("p (c i) t -> p c t i", i=4),
        in_=raw[:, :, c0:c1].rearrange("p t (c i) -> p c t i", i=4),
    )


def spans(widths):
    return [slice(sum(widths[:n]), sum(widths[: n + 1])) for n in range(len(widths))]


def tile_attend_bsharedprefix_heads_kernel(tc, query, keys_words, keys_scales, gout, vals, zp, cp, old, offs, out):
    nc = tc.nc
    with ExitStack() as ctx:
        keep = ctx.enter_context(tc.tile_pool(name="keep", bufs=1))
        psum = ctx.enter_context(tc.psum_pool(name="psum", bufs=1))

        offsets = keep.tile([P, SLOTS // 16], U16, name="offsets")
        key_scales = keep.tile([P, T], U8, name="key_scales", align_bytes=64)
        placed = keep.tile([P, T], F32, name="placed")
        p_ext = keep.tile([P, SLOTS + 4], F32, name="p_ext")
        c_ext = keep.tile([P, SLOTS + 4], F32, name="c_ext")
        q_raw = keep.tile([P, PACK, Q], F32, name="q_raw")
        g_raw = keep.tile([P, PACK, Q], F32, name="g_raw")
        val_cols = spans(VAL_CHUNKS)
        key_cols = spans(KEY_CHUNKS)
        key_codes = keep.tile([P, T], U32, name="key_codes", align_bytes=64)
        v_raw = [keep.tile([P, PACK, w], F32, name="v_raw%d" % n) for n, w in enumerate(VAL_CHUNKS)]
        old_sb = keep.tile([P, T], F32, name="old_sb")

        scale_rows = keep.tile([P, T // 4], I32, name="scale_rows")
        nc.vector.memset(key_scales[:].bitcast(I32), 0)
        nc.vector.memset(placed[:], 0.0)
        nc.gpsimd.memset(p_ext[:, SLOTS:], 1.0)
        nc.gpsimd.memset(c_ext[:, SLOTS:], 0.0)

        def load_vals(n):
            nc.sync.dma_start(out=v_raw[n][:], in_=vals[:, val_cols[n]].rearrange("(p j) w -> p j w", j=PACK))

        key_words = keys_words[0].rearrange("p n t -> p (n t)").bitcast(I32)

        def load_keys(n):
            nc.sync.dma_start(out=key_codes[:].bitcast(I32), in_=key_words)

        def load_scales():
            for quad in range(4):
                nc.sync.dma_start(
                    out=scale_rows[32 * quad : 32 * quad + 4, :],
                    in_=keys_scales[0, 4 * quad : 4 * quad + 4, :].bitcast(I32),
                )

        def load_prefix():
            with nc.allow_non_contiguous_dma(reason="one value a partition"):
                nc.gpsimd.dma_start(out=p_ext[:, SLOTS : SLOTS + 1], in_=zp)
                nc.gpsimd.dma_start(out=c_ext[:, SLOTS + 1 : SLOTS + 2], in_=cp)

        load_prefix()
        nc.sync.dma_start(offsets[:], offs)
        nc.sync.dma_start(out=q_raw[:], in_=query.rearrange("(p j) w -> p j w", j=PACK))
        load_scales()
        load_keys(0)
        nc.sync.dma_start(out=g_raw[:], in_=gout.rearrange("(p j) w -> p j w", j=PACK))
        load_vals(0)
        load_vals(1)
        load_vals(2)
        load_vals(3)
        load_vals(4)
        nc.sync.dma_start(out=old_sb[:], in_=old)

        for quad in range(4):
            rows = slice(32 * quad, 32 * quad + 4)
            nc.vector.tensor_copy(out=key_scales[rows, :].bitcast(I32), in_=scale_rows[rows, :])

        def operand(name, width, codes_tag=None):
            grouped = keep.tile([P, width, PACK], BF16, name=name + "_grouped", tag=name + "_grouped", align_bytes=64)
            codes = keep.tile([P, width], U32, name=name + "_codes", tag=codes_tag or name + "_codes", align_bytes=64)
            scales = keep.tile([P, width], U8, name=name + "_scales", align_bytes=64)
            return grouped, codes, scales

        def quantize(grouped, codes, scales):
            nc.vector.quantize_mx(
                out=codes[:].bitcast(FP8X4), scales=scales[:], in_=grouped[:].rearrange("p w j -> p (w j)")
            )

        g_op = operand("g", Q)
        q_op = operand("q", Q)
        c_all = keep.tile([P, T], F32, name="c_all")
        a_all = keep.tile([P, T], F32, name="a_all")

        def stationary(op, raw, copy):
            interleave(copy, op[0], raw, 0, Q)
            quantize(*op)

        v_ops = {}

        def value_prepare(n):
            w = VAL_CHUNKS[n]
            v_ops[n] = operand("v%d" % n, w, CODE_TAGS.get(n))
            grouped, codes, scales = v_ops[n]
            for half in range(2):
                interleave(nc.vector.tensor_copy, grouped, v_raw[n], half * w // 2, (half + 1) * w // 2)

        def value_quantize(n):
            grouped, codes, scales = v_ops[n]
            w = VAL_CHUNKS[n]
            for half in range(2):
                cols = slice(half * w // 2, (half + 1) * w // 2)
                nc.vector.quantize_mx(
                    out=codes[:, cols].bitcast(FP8X4), scales=scales[:, cols],
                    in_=grouped[:, cols, :].rearrange("p w j -> p (w j)"),
                )

        def value_pair(n, drain):
            w = VAL_CHUNKS[n]
            acc = psum.tile([P, 2 * w], F32, name="acc", tag=C_BANKS[n])
            for m in range(2):
                grouped, codes, scales = v_ops[n + m]
                nc.tensor.matmul_mx(
                    out=acc[:, m * w : (m + 1) * w], lhsT=g_op[1][:].bitcast(FP8X4), lhsT_scale=g_op[2][:],
                    rhs=codes[:].bitcast(FP8X4), rhs_scale=scales[:], start=True, stop=True,
                )
            drain(out=c_all[:, val_cols[n].start : val_cols[n + 1].stop], in_=acc[:])

        def value_chunk(n, drain):
            w = VAL_CHUNKS[n]
            grouped, codes, scales = v_ops[n]
            acc = psum.tile([P, w], F32, name="acc", tag=C_BANKS[n])
            nc.tensor.matmul_mx(
                out=acc[:], lhsT=g_op[1][:].bitcast(FP8X4), lhsT_scale=g_op[2][:],
                rhs=codes[:].bitcast(FP8X4), rhs_scale=scales[:], start=True, stop=True,
            )
            drain(out=c_all[:, val_cols[n]], in_=acc[:])

        def key_chunk(n, drain):
            acc = psum.tile([P, KEY_CHUNKS[n]], F32, name="acc", tag=A_BANKS[n])
            nc.tensor.matmul_mx(
                out=acc[:], lhsT=q_op[1][:].bitcast(FP8X4), lhsT_scale=q_op[2][:],
                rhs=key_codes[:, key_cols[n]].bitcast(FP8X4), rhs_scale=key_scales[:, key_cols[n]], start=True, stop=True,
            )
            drain(out=a_all[:, key_cols[n]], in_=acc[:])

        z = keep.tile([P, 1], F32, name="z")
        z_terms = keep.tile([P, SLOTS + 1], F32, name="z_terms")

        def exponentials():
            nc.scalar.activation(out=p_ext[:, :SLOTS], in_=a_all[:].indirect(offsets[:]), func=ACT.Exp)
            nc.scalar.activation(out=z_terms[:], in_=p_ext[:, : SLOTS + 1], func=ACT.Copy, accum_out=z[:])

        def look_up_c():
            nc.vector.tensor_copy(out=c_ext[:, :SLOTS], in_=c_all[:].indirect(offsets[:]))

        stationary(q_op, q_raw, nc.scalar.copy)
        key_chunk(0, nc.scalar.copy)
        key_chunk(1, nc.scalar.copy)
        stationary(g_op, g_raw, nc.vector.tensor_copy)
        exponentials()
        value_prepare(0)
        value_quantize(0)
        value_chunk(0, nc.scalar.copy)
        value_prepare(1)
        value_quantize(1)
        value_chunk(1, nc.scalar.copy)
        value_prepare(2)
        value_quantize(2)
        value_chunk(2, nc.scalar.copy)
        value_prepare(3)
        value_quantize(3)
        value_chunk(3, nc.scalar.copy)
        value_prepare(4)
        value_quantize(4)
        value_chunk(4, nc.scalar.copy)


        inv_z = keep.tile([P, 1], F32, name="inv_z", tag="v4_grouped", align_bytes=64)
        neg_m = keep.tile([P, 1], F32, name="neg_m")
        m_terms = keep.tile([P, SLOTS + 2], F32, name="m_terms")
        centred = keep.tile([P, SLOTS], F32, name="centred")
        weight = keep.tile([P, SLOTS + 2], F32, name="weight")
        nc.vector.reciprocal(out=inv_z[:], in_=z[:])
        nc.vector.tensor_scalar(
            out=weight[:], in0=p_ext[:, : SLOTS + 2], scalar1=inv_z[:], scalar2=None, op0=ALU.mult
        )
        look_up_c()
        nc.vector.scalar_tensor_tensor(
            out=m_terms[:], in0=weight[:], scalar=-1.0, in1=c_ext[:, : SLOTS + 2],
            op0=ALU.mult, op1=ALU.mult, accum_out=neg_m[:],
        )
        nc.vector.tensor_scalar(
            out=centred[:], in0=c_ext[:, :SLOTS], scalar1=neg_m[:], scalar2=None, op0=ALU.add
        )
        nc.vector.tensor_tensor(
            out=placed[:].indirect(offsets[:]), in0=centred[:], in1=weight[:, :SLOTS], op=ALU.mult
        )

        for n, cols in enumerate(spans(STORE_CHUNKS)):
            result = keep.tile([P, STORE_CHUNKS[n]], F32, name="result%d" % n)
            nc.vector.scalar_tensor_tensor(
                out=result[:], in0=placed[:, cols], scalar=GAIN, in1=old_sb[:, cols], op0=ALU.mult, op1=ALU.add
            )
            (nc.sync if n % 2 == 0 else nc.scalar).dma_start(out=out[:, cols], in_=result[:])
